import numpy as np
import ml_dtypes


def mxq(x, axis, fmt="e4m3"):
    dtype, down = {"e4m3": (ml_dtypes.float8_e4m3fn, 7), "e5m2": (ml_dtypes.float8_e5m2, 14)}[fmt]
    v = np.moveaxis(np.asarray(x, np.float32).astype(ml_dtypes.bfloat16).astype(np.float64), axis, -1)
    blocks = v.reshape(v.shape[:-1] + (-1, 32))
    amax = np.abs(blocks).max(-1, keepdims=True)
    byte = np.maximum(np.where(amax > 0, np.frexp(amax)[1] - 1 + 127, 0) - down, 1)
    scale = np.exp2(byte - 127.0)
    codes = (blocks / scale).astype(np.float32).astype(dtype).astype(np.float64)
    return np.moveaxis((codes * scale).reshape(v.shape), -1, axis)


WIDE = False


def mx_kscale(k, group=512):
    if not WIDE:
        return np.ones(k)
    levels = np.array([10, -10, 5, -5, 0])
    if group != 512:
        return np.exp2(np.random.permutation(np.resize(levels, k // group))).repeat(group)
    if k % 512:
        return np.exp2(np.random.permutation(np.resize(levels, k // 32))).repeat(32)
    a = np.empty((k // 512, 16))
    for p in range(k // 512):
        a[p, :8] = np.random.permutation(np.resize(levels, 8))
        for g in range(8):
            far = levels[np.abs(levels - a[p, g]) >= 10]
            a[p, g + 8] = far[np.random.randint(len(far))]
    return np.exp2(a.ravel()).repeat(32)


def f64(x):
    return np.asarray(x).astype(np.float64)


H, D, N = 4, 256, 1024


def setup_inputs():
    n = np.random.standard_normal
    s = mx_kscale(D, 0)[:, None]
    S = n((H, D, 128))
    S[:, :, 127] = np.random.uniform(0.5, 1.5, (H, D))
    return {
        "q": n((H, D, N)).astype(np.float32),
        "qa": (np.random.uniform(0.5, 2.0, (D, 1)) * s).astype(np.float32),
        "S": (S / s).astype(np.float32),
    }


def reference(q, qa, S):
    fq = (1.0 / (1.0 + np.exp(-f64(q)))) * f64(qa)
    y = mxq(fq, 1, "e4m3").transpose(0, 2, 1) @ mxq(f64(S), 1, "e4m3")
    y = y / y[:, :, 127:128]
    return y

@@ -1,0 +1,231 @@
+from contextlib import ExitStack
+
+import concourse.mybir as mybir
+
+H, D, N, E = 4, 256, 1024, 128
+FLOPS = 2 * H * D * N * E
+
+F32 = mybir.dt.float32
+BF16 = mybir.dt.bfloat16
+U32 = mybir.dt.uint32
+U8 = mybir.dt.uint8
+FP8X4 = mybir.dt.float8_e4m3fn_x4
+ACT = mybir.ActivationFunctionType
+ALU = mybir.AluOpType
+
+P = 128
+ROWS = 64
+PACK = 4
+M = 128
+
+CHUNKS = [
+    (0, 0, 256, True),
+    (0, 256, 256, True),
+    (0, 512, 256, False),
+    (0, 768, 256, False),
+    (1, 0, 512, True),
+    (1, 512, 512, True),
+]
+
+
+def tile_rows_read_sig_norm_kernel(tc, q, qa, S, out):
+    nc = tc.nc
+    q_rows = q.rearrange("(g c) (p j) n -> g (c p) j n", c=2, j=PACK)
+    s_rows = S.rearrange("(g c) (p j) e -> g (c p) j e", c=2, j=PACK)
+
+    with ExitStack() as ctx:
+        sb = ctx.enter_context(tc.tile_pool(name="sb", bufs=1))
+        ps = ctx.enter_context(tc.psum_pool(name="ps", bufs=1))
+        ctx.enter_context(tc.manual_schedule())
+
+        qa_t = sb.tile([P, 8], F32, name="qa_t")
+        qa_rows = qa.rearrange("(p j) o -> p (j o)", j=PACK)
+        for c in range(2):
+            nc.scalar.dma_start(out=qa_t[ROWS * c : ROWS * (c + 1), 0:PACK], in_=qa_rows)
+        qa_b = qa_t[:, 0:PACK].rearrange("p (u e) -> p u e", e=2).unsqueeze(1).to_broadcast([P, M, 2, 2])
+
+        raw = {}
+        s_raw = {}
+
+        def load_q(k):
+            g, n0, w, split = CHUNKS[k]
+            if split:
+                for u in range(2):
+                    t = sb.tile([P, 2, w], F32, name="raw%d_%d" % (k, u))
+                    nc.sync.dma_start(out=t[:], in_=q_rows[g, :, 2 * u : 2 * u + 2, n0 : n0 + w])
+                    raw[k, u] = t
+            else:
+                t = sb.tile([P, PACK, w], F32, name="raw%d" % k)
+                nc.sync.dma_start(out=t[:], in_=q_rows[g, :, :, n0 : n0 + w])
+                raw[k, 0] = t
+
+        def load_s(g):
+            t = sb.tile([P, PACK, E], F32, name="s_raw%d" % g)
+            nc.sync.dma_start(out=t[:], in_=s_rows[g])
+            s_raw[g] = t
+
+        load_q(0)
+        load_q(1)
+        load_s(0)
+        load_q(2)
+        load_q(3)
+        load_q(4)
+        load_s(1)
+        load_q(5)
+
+        sig = {k: sb.tile([P, 2, CHUNKS[k][2], 2], F32, name="sig%d" % k) for k in range(len(CHUNKS))}
+        res = {k: sb.tile([P, 2, CHUNKS[k][2] // M, E], F32, name="res%d" % k) for k in range(len(CHUNKS))}
+
+        def sigmoid(k, u):
+            if CHUNKS[k][3]:
+                nc.scalar.activation(out=sig[k][:, u, :, :], in_=raw[k, u][:].rearrange("p e n -> p n e"), func=ACT.Sigmoid)
+            else:
+                nc.scalar.activation(out=sig[k][:], in_=raw[k, 0][:].rearrange("p (u e) n -> p u n e", e=2), func=ACT.Sigmoid)
+
+        s_bf, s_codes, s_scales = {}, {}, {}
+
+        def s_round(g, eng):
+            t = sb.tile([P, E, PACK], BF16, name="s_bf%d" % g, align_bytes=64)
+            o = t[:].rearrange("p (c i) j -> p c j i", i=2)
+            i_ = s_raw[g][:].rearrange("p j (c i) -> p c j i", i=2)
+            if eng == "s":
+                nc.scalar.copy(out=o, in_=i_)
+            else:
+                nc.vector.tensor_copy(out=o, in_=i_)
+            s_bf[g] = t
+
+        def s_quant(g):
+            s_codes[g] = sb.tile([P, E], U32, name="s_codes%d" % g, align_bytes=64)
+            s_scales[g] = sb.tile([P, E], U8, name="s_scales%d" % g, align_bytes=64)
+            nc.vector.quantize_mx(out=s_codes[g][:].bitcast(FP8X4), scales=s_scales[g][:], in_=s_bf[g][:].rearrange("p e j -> p (e j)"))
+
+        units = []
+        for k, (g, n0, w, split) in enumerate(CHUNKS):
+            for r0 in range(0, w // M, 2):
+                units.append((k, r0))
+        fq = {t: sb.tile([P, 2, M, 2, 2], BF16, name="fq%d" % t, align_bytes=64) for t in range(len(units))}
+        codes, scales, acc, inv = {}, {}, {}, {}
+
+        def mult(t, i):
+            k, r0 = units[t]
+            nr = CHUNKS[k][2] // M
+            src = sig[k][:].rearrange("p u (m r) e -> p r m u e", r=nr)[:, r0 + i, :, :, :]
+            nc.vector.tensor_tensor(out=fq[t][:, i, :, :, :], in0=src, in1=qa_b, op=ALU.mult)
+
+        def quant_mm(t):
+            k, r0 = units[t]
+            g = CHUNKS[k][0]
+            codes[t] = sb.tile([P, 2 * M], U32, name="codes%d" % t, align_bytes=64)
+            scales[t] = sb.tile([P, 2 * M], U8, name="scales%d" % t, align_bytes=64)
+            nc.vector.quantize_mx(out=codes[t][:].bitcast(FP8X4), scales=scales[t][:], in_=fq[t][:].rearrange("p i m u e -> p (i m u e)"))
+
+        def mm(t):
+            k, r0 = units[t]
+            g = CHUNKS[k][0]
+            for c in range(2):
+                acc[t, c] = ps.tile([P, 4, E], F32, name="acc%d_%d" % (t, c), tag="acc%d_%d" % (t % 4, c))
+            for i in range(2):
+                for c in range(2):
+                    rows = slice(ROWS * c, ROWS * (c + 1))
+                    cols = slice(M * i, M * (i + 1))
+                    nc.tensor.matmul_mx(
+                        out=acc[t, c][:, i, :],
+                        lhsT=codes[t][rows, cols].bitcast(FP8X4),
+                        lhsT_scale=scales[t][rows, cols],
+                        rhs=s_codes[g][rows, :].bitcast(FP8X4),
+                        rhs_scale=s_scales[g][rows, :],
+                        start=True,
+                        stop=True,
+                    )
+
+        def recip(t):
+            for c in range(2):
+                inv[t, c] = sb.tile([P, 8], F32, name="inv%d_%d" % (t, c))
+                nc.vector.reciprocal(out=inv[t, c][:, 0:2], in_=acc[t, c][:, 0:2, E - 1])
+
+        def evac_s(t, c):
+            k, r0 = units[t]
+            for i in range(2):
+                nc.scalar.activation(out=res[k][:, c, r0 + i, :], in_=acc[t, c][:, i, :], func=ACT.Copy, scale=inv[t, c][:, i : i + 1])
+
+        def evac_v(t, c):
+            k, r0 = units[t]
+            nc.vector.tensor_tensor(
+                out=res[k][:, c, r0 : r0 + 2, :],
+                in0=acc[t, c][:, 0:2, :],
+                in1=inv[t, c][:, 0:2].unsqueeze(2).to_broadcast([P, 2, E]),
+                op=ALU.mult,
+            )
+
+        def store(k, r0, r1):
+            g, n0, w, split = CHUNKS[k]
+            nr = w // M
+            dst = out[2 * g : 2 * g + 2, n0 : n0 + w, :].rearrange("c (m r) e -> m c r e", r=nr)[:, :, r0:r1, :]
+            nc.sync.dma_start(out=dst.rearrange("m c r e -> m c (r e)"), in_=res[k][:, :, r0:r1, :].rearrange("m c r e -> m c (r e)"))
+
+        def evac(t):
+            evac_s(t, 0)
+            evac_s(t, 1)
+
+        sigmoid(0, 0)
+        sigmoid(0, 1)
+        sigmoid(1, 0)
+        sigmoid(1, 1)
+        s_round(0, "s")
+        sigmoid(2, 0)
+        sigmoid(3, 0)
+        mult(0, 0)
+        mult(0, 1)
+        mult(1, 0)
+        quant_mm(0)
+        mult(1, 1)
+        s_quant(0)
+        mm(0)
+        mult(2, 0)
+        quant_mm(1)
+        mm(1)
+        recip(0)
+        evac(0)
+        store(0, 0, 2)
+        sigmoid(4, 0)
+        sigmoid(4, 1)
+        mult(2, 1)
+        mult(3, 0)
+        quant_mm(2)
+        mm(2)
+        recip(1)
+        evac(1)
+        store(1, 0, 2)
+        sigmoid(5, 0)
+        sigmoid(5, 1)
+        mult(3, 1)
+        s_round(1, "v")
+        quant_mm(3)
+        mm(3)
+        recip(2)
+        evac(2)
+        store(2, 0, 2)
+        mult(4, 0)
+        s_quant(1)
+        mult(4, 1)
+        for t in range(5, 8):
+            mult(t, 0)
+            quant_mm(t - 1)
+            recip(t - 2)
+            evac(t - 2)
+            mm(t - 1)
+            mult(t, 1)
+            if t == 5:
+                store(3, 0, 2)
+            if t == 7:
+                store(4, 0, 4)
+        recip(6)
+        quant_mm(7)
+        mm(7)
+        evac_s(6, 0)
+        evac_v(6, 1)
+        store(5, 0, 2)
+        recip(7)
+        evac_s(7, 0)
+        evac_v(7, 1)
+        store(5, 2, 4)

@@ -14,218 +14,147 @@ ACT = mybir.ActivationFunctionType
 ALU = mybir.AluOpType
 
 P = 128
-ROWS = 64
+SIDE = 2
+ROWS = P // SIDE
 PACK = 4
 M = 128
-
-CHUNKS = [
-    (0, 0, 256, True),
-    (0, 256, 256, True),
-    (0, 512, 256, False),
-    (0, 768, 256, False),
-    (1, 0, 512, True),
-    (1, 512, 512, True),
-]
+DEAL = 2
+CHUNK = M * DEAL
+CHUNKS_PER_PAIR = N // CHUNK
+CHUNKS = (H // SIDE) * CHUNKS_PER_PAIR
+BANKS = 4
+STATE_AT = 2
+AHEAD = 4
+LAG = 2
 
 
 def tile_rows_read_sig_norm_kernel(tc, q, qa, S, out):
     nc = tc.nc
-    q_rows = q.rearrange("(g c) (p j) n -> g (c p) j n", c=2, j=PACK)
-    s_rows = S.rearrange("(g c) (p j) e -> g (c p) j e", c=2, j=PACK)
+    q_rows = q.rearrange("(g c) (p u e) n -> g (c p) u e n", c=SIDE, u=2, e=2)
+    s_rows = S.rearrange("(g c) (p j) e -> g (c p) j e", c=SIDE, j=PACK)
+    qa_rows = qa.rearrange("(p j) o -> p (j o)", j=PACK)
+
+    batches = [(k, 0, DEAL) for k in range(CHUNKS - 1)] + [(CHUNKS - 1, r, 1) for r in range(DEAL)]
+    last = len(batches) - 1
 
     with ExitStack() as ctx:
         sb = ctx.enter_context(tc.tile_pool(name="sb", bufs=1))
         ps = ctx.enter_context(tc.psum_pool(name="ps", bufs=1))
         ctx.enter_context(tc.manual_schedule())
 
-        qa_t = sb.tile([P, 8], F32, name="qa_t")
-        qa_rows = qa.rearrange("(p j) o -> p (j o)", j=PACK)
-        for c in range(2):
-            nc.scalar.dma_start(out=qa_t[ROWS * c : ROWS * (c + 1), 0:PACK], in_=qa_rows)
-        qa_b = qa_t[:, 0:PACK].rearrange("p (u e) -> p u e", e=2).unsqueeze(1).to_broadcast([P, M, 2, 2])
+        qa_t = sb.tile([P, PACK], F32, name="qa_t")
+        for c in range(SIDE):
+            nc.scalar.dma_start(out=qa_t[ROWS * c : ROWS * (c + 1), :], in_=qa_rows)
+        qa_cols = qa_t[:].rearrange("p (u e) -> p u e", e=2).unsqueeze(1).to_broadcast([P, M, 2, 2])
 
-        raw = {}
-        s_raw = {}
+        q_raw, s_raw = {}, {}
+        for k in range(CHUNKS):
+            g, n0 = k // CHUNKS_PER_PAIR, CHUNK * (k % CHUNKS_PER_PAIR)
+            if k % CHUNKS_PER_PAIR == STATE_AT:
+                s_raw[g] = sb.tile([P, PACK, E], F32, name="s_raw%d" % g)
+                nc.sync.dma_start(out=s_raw[g][:], in_=s_rows[g])
+            for u in range(2):
+                q_raw[k, u] = sb.tile([P, 2, CHUNK], F32, name="q_raw%d_%d" % (k, u))
+                nc.sync.dma_start(out=q_raw[k, u][:], in_=q_rows[g, :, u, :, n0 : n0 + CHUNK])
 
-        def load_q(k):
-            g, n0, w, split = CHUNKS[k]
-            if split:
-                for u in range(2):
-                    t = sb.tile([P, 2, w], F32, name="raw%d_%d" % (k, u))
-                    nc.sync.dma_start(out=t[:], in_=q_rows[g, :, 2 * u : 2 * u + 2, n0 : n0 + w])
-                    raw[k, u] = t
-            else:
-                t = sb.tile([P, PACK, w], F32, name="raw%d" % k)
-                nc.sync.dma_start(out=t[:], in_=q_rows[g, :, :, n0 : n0 + w])
-                raw[k, 0] = t
+        phi, s_bf, s_codes, s_scales = {}, {}, {}, {}
+        fq, codes, scales, acc, inv, res = {}, {}, {}, {}, {}, {}
 
-        def load_s(g):
-            t = sb.tile([P, PACK, E], F32, name="s_raw%d" % g)
-            nc.sync.dma_start(out=t[:], in_=s_rows[g])
-            s_raw[g] = t
+        def feature_map(k):
+            g = k // CHUNKS_PER_PAIR
+            if k % CHUNKS_PER_PAIR == STATE_AT:
+                s_bf[g] = sb.tile([P, E, PACK], BF16, name="s_bf%d" % g, align_bytes=64)
+                nc.scalar.copy(
+                    out=s_bf[g][:].rearrange("p (x i) j -> p x j i", i=2),
+                    in_=s_raw[g][:].rearrange("p j (x i) -> p x j i", i=2),
+                )
+            phi[k] = sb.tile([P, 2, CHUNK, 2], F32, name="phi%d" % k)
+            for u in range(2):
+                nc.scalar.activation(out=phi[k][:, u, :, :], in_=q_raw[k, u][:].rearrange("p e n -> p n e"), func=ACT.Sigmoid)
 
-        load_q(0)
-        load_q(1)
-        load_s(0)
-        load_q(2)
-        load_q(3)
-        load_q(4)
-        load_s(1)
-        load_q(5)
+        def weigh(b, i):
+            k, r0, count = batches[b]
+            if i == 0:
+                fq[b] = sb.tile([P, count, M, 2, 2], BF16, name="fq%d" % b, align_bytes=64)
+            dealt = phi[k][:].rearrange("p u (m r) e -> p r m u e", r=DEAL)
+            nc.vector.tensor_tensor(out=fq[b][:, i, :, :, :], in0=dealt[:, r0 + i, :, :, :], in1=qa_cols, op=ALU.mult)
 
-        sig = {k: sb.tile([P, 2, CHUNKS[k][2], 2], F32, name="sig%d" % k) for k in range(len(CHUNKS))}
-        res = {k: sb.tile([P, 2, CHUNKS[k][2] // M, E], F32, name="res%d" % k) for k in range(len(CHUNKS))}
-
-        def sigmoid(k, u):
-            if CHUNKS[k][3]:
-                nc.scalar.activation(out=sig[k][:, u, :, :], in_=raw[k, u][:].rearrange("p e n -> p n e"), func=ACT.Sigmoid)
-            else:
-                nc.scalar.activation(out=sig[k][:], in_=raw[k, 0][:].rearrange("p (u e) n -> p u n e", e=2), func=ACT.Sigmoid)
-
-        s_bf, s_codes, s_scales = {}, {}, {}
-
-        def s_round(g, eng):
-            t = sb.tile([P, E, PACK], BF16, name="s_bf%d" % g, align_bytes=64)
-            o = t[:].rearrange("p (c i) j -> p c j i", i=2)
-            i_ = s_raw[g][:].rearrange("p j (c i) -> p c j i", i=2)
-            if eng == "s":
-                nc.scalar.copy(out=o, in_=i_)
-            else:
-                nc.vector.tensor_copy(out=o, in_=i_)
-            s_bf[g] = t
-
-        def s_quant(g):
+        def quantize_state(g):
             s_codes[g] = sb.tile([P, E], U32, name="s_codes%d" % g, align_bytes=64)
             s_scales[g] = sb.tile([P, E], U8, name="s_scales%d" % g, align_bytes=64)
             nc.vector.quantize_mx(out=s_codes[g][:].bitcast(FP8X4), scales=s_scales[g][:], in_=s_bf[g][:].rearrange("p e j -> p (e j)"))
 
-        units = []
-        for k, (g, n0, w, split) in enumerate(CHUNKS):
-            for r0 in range(0, w // M, 2):
-                units.append((k, r0))
-        fq = {t: sb.tile([P, 2, M, 2, 2], BF16, name="fq%d" % t, align_bytes=64) for t in range(len(units))}
-        codes, scales, acc, inv = {}, {}, {}, {}
+        def quantize_queries(b):
+            count = batches[b][2]
+            codes[b] = sb.tile([P, count * M], U32, name="codes%d" % b, align_bytes=64)
+            scales[b] = sb.tile([P, count * M], U8, name="scales%d" % b, align_bytes=64)
+            nc.vector.quantize_mx(out=codes[b][:].bitcast(FP8X4), scales=scales[b][:], in_=fq[b][:].rearrange("p i m u e -> p (i m u e)"))
 
-        def mult(t, i):
-            k, r0 = units[t]
-            nr = CHUNKS[k][2] // M
-            src = sig[k][:].rearrange("p u (m r) e -> p r m u e", r=nr)[:, r0 + i, :, :, :]
-            nc.vector.tensor_tensor(out=fq[t][:, i, :, :, :], in0=src, in1=qa_b, op=ALU.mult)
-
-        def quant_mm(t):
-            k, r0 = units[t]
-            g = CHUNKS[k][0]
-            codes[t] = sb.tile([P, 2 * M], U32, name="codes%d" % t, align_bytes=64)
-            scales[t] = sb.tile([P, 2 * M], U8, name="scales%d" % t, align_bytes=64)
-            nc.vector.quantize_mx(out=codes[t][:].bitcast(FP8X4), scales=scales[t][:], in_=fq[t][:].rearrange("p i m u e -> p (i m u e)"))
-
-        def mm(t):
-            k, r0 = units[t]
-            g = CHUNKS[k][0]
-            for c in range(2):
-                acc[t, c] = ps.tile([P, 4, E], F32, name="acc%d_%d" % (t, c), tag="acc%d_%d" % (t % 4, c))
-            for i in range(2):
-                for c in range(2):
+        def multiply(b):
+            k, r0, count = batches[b]
+            g = k // CHUNKS_PER_PAIR
+            for c in range(SIDE):
+                acc[b, c] = ps.tile([P, count, E], F32, name="acc%d_%d" % (b, c), tag="bank%d_%d" % (b % BANKS, c))
+            for c in range(SIDE):
+                for i in range(count):
                     rows = slice(ROWS * c, ROWS * (c + 1))
                     cols = slice(M * i, M * (i + 1))
                     nc.tensor.matmul_mx(
-                        out=acc[t, c][:, i, :],
-                        lhsT=codes[t][rows, cols].bitcast(FP8X4),
-                        lhsT_scale=scales[t][rows, cols],
+                        out=acc[b, c][:, i, :],
+                        lhsT=codes[b][rows, cols].bitcast(FP8X4),
+                        lhsT_scale=scales[b][rows, cols],
                         rhs=s_codes[g][rows, :].bitcast(FP8X4),
                         rhs_scale=s_scales[g][rows, :],
                         start=True,
                         stop=True,
                     )
 
-        def recip(t):
-            for c in range(2):
-                inv[t, c] = sb.tile([P, 8], F32, name="inv%d_%d" % (t, c))
-                nc.vector.reciprocal(out=inv[t, c][:, 0:2], in_=acc[t, c][:, 0:2, E - 1])
+        def invert(b):
+            count = batches[b][2]
+            for c in range(SIDE):
+                inv[b, c] = sb.tile([P, count], F32, name="inv%d_%d" % (b, c))
+                nc.vector.reciprocal(out=inv[b, c][:], in_=acc[b, c][:, :, E - 1])
 
-        def evac_s(t, c):
-            k, r0 = units[t]
-            for i in range(2):
-                nc.scalar.activation(out=res[k][:, c, r0 + i, :], in_=acc[t, c][:, i, :], func=ACT.Copy, scale=inv[t, c][:, i : i + 1])
+        def normalise(b, share):
+            k, r0, count = batches[b]
+            if r0 == 0:
+                res[k] = sb.tile([P, SIDE, DEAL, E], F32, name="res%d" % k)
+            for c in range(1 if share else SIDE):
+                for i in range(count):
+                    nc.scalar.activation(out=res[k][:, c, r0 + i, :], in_=acc[b, c][:, i, :], func=ACT.Copy, scale=inv[b, c][:, i : i + 1])
+            if share:
+                nc.vector.tensor_tensor(
+                    out=res[k][:, 1, r0 : r0 + count, :],
+                    in0=acc[b, 1][:],
+                    in1=inv[b, 1][:].unsqueeze(2).to_broadcast([P, count, E]),
+                    op=ALU.mult,
+                )
+            if r0 + count == DEAL:
+                g, n0 = k // CHUNKS_PER_PAIR, CHUNK * (k % CHUNKS_PER_PAIR)
+                rows = out[SIDE * g : SIDE * (g + 1), n0 : n0 + CHUNK, :]
+                nc.sync.dma_start(out=rows.rearrange("c (m r) e -> m c (r e)", r=DEAL), in_=res[k][:].rearrange("m c r e -> m c (r e)"))
 
-        def evac_v(t, c):
-            k, r0 = units[t]
-            nc.vector.tensor_tensor(
-                out=res[k][:, c, r0 : r0 + 2, :],
-                in0=acc[t, c][:, 0:2, :],
-                in1=inv[t, c][:, 0:2].unsqueeze(2).to_broadcast([P, 2, E]),
-                op=ALU.mult,
-            )
-
-        def store(k, r0, r1):
-            g, n0, w, split = CHUNKS[k]
-            nr = w // M
-            dst = out[2 * g : 2 * g + 2, n0 : n0 + w, :].rearrange("c (m r) e -> m c r e", r=nr)[:, :, r0:r1, :]
-            nc.sync.dma_start(out=dst.rearrange("m c r e -> m c (r e)"), in_=res[k][:, :, r0:r1, :].rearrange("m c r e -> m c (r e)"))
-
-        def evac(t):
-            evac_s(t, 0)
-            evac_s(t, 1)
-
-        sigmoid(0, 0)
-        sigmoid(0, 1)
-        sigmoid(1, 0)
-        sigmoid(1, 1)
-        s_round(0, "s")
-        sigmoid(2, 0)
-        sigmoid(3, 0)
-        mult(0, 0)
-        mult(0, 1)
-        mult(1, 0)
-        quant_mm(0)
-        mult(1, 1)
-        s_quant(0)
-        mm(0)
-        mult(2, 0)
-        quant_mm(1)
-        mm(1)
-        recip(0)
-        evac(0)
-        store(0, 0, 2)
-        sigmoid(4, 0)
-        sigmoid(4, 1)
-        mult(2, 1)
-        mult(3, 0)
-        quant_mm(2)
-        mm(2)
-        recip(1)
-        evac(1)
-        store(1, 0, 2)
-        sigmoid(5, 0)
-        sigmoid(5, 1)
-        mult(3, 1)
-        s_round(1, "v")
-        quant_mm(3)
-        mm(3)
-        recip(2)
-        evac(2)
-        store(2, 0, 2)
-        mult(4, 0)
-        s_quant(1)
-        mult(4, 1)
-        for t in range(5, 8):
-            mult(t, 0)
-            quant_mm(t - 1)
-            recip(t - 2)
-            evac(t - 2)
-            mm(t - 1)
-            mult(t, 1)
-            if t == 5:
-                store(3, 0, 2)
-            if t == 7:
-                store(4, 0, 4)
-        recip(6)
-        quant_mm(7)
-        mm(7)
-        evac_s(6, 0)
-        evac_v(6, 1)
-        store(5, 0, 2)
-        recip(7)
-        evac_s(7, 0)
-        evac_v(7, 1)
-        store(5, 2, 4)
+        for k in range(AHEAD):
+            feature_map(k)
+        for b in range(last + 1):
+            weigh(b, 0)
+            if b >= 1:
+                quantize_queries(b - 1)
+            if b % CHUNKS_PER_PAIR == 1:
+                quantize_state(b // CHUNKS_PER_PAIR)
+            if LAG <= b < last:
+                invert(b - LAG)
+                normalise(b - LAG, False)
+            if b + AHEAD < CHUNKS:
+                feature_map(b + AHEAD)
+            if b >= 1:
+                multiply(b - 1)
+            for i in range(1, batches[b][2]):
+                weigh(b, i)
+        quantize_queries(last)
+        multiply(last)
+        invert(last - LAG)
+        for b in range(last - LAG, last + 1):
+            if b < last:
+                invert(b + 1)
+            normalise(b, True)

@@ -24,7 +24,7 @@ CHUNKS_PER_PAIR = N // CHUNK
 CHUNKS = (H // SIDE) * CHUNKS_PER_PAIR
 BANKS = 4
 STATE_AT = 2
-AHEAD = 4
+AHEAD = 3
 LAG = 2
 
 
@@ -32,7 +32,7 @@ def tile_rows_read_sig_norm_kernel(tc, q, qa, S, out):
     nc = tc.nc
     q_rows = q.rearrange("(g c) (p u e) n -> g (c p) u e n", c=SIDE, u=2, e=2)
     s_rows = S.rearrange("(g c) (p j) e -> g (c p) j e", c=SIDE, j=PACK)
-    qa_rows = qa.rearrange("(p j) o -> p (j o)", j=PACK)
+    qa_rows = qa.rearrange("(p j) o -> p (j o)", j=PACK).unsqueeze(0).to_broadcast([SIDE, ROWS, PACK])
 
     batches = [(k, 0, DEAL) for k in range(CHUNKS - 1)] + [(CHUNKS - 1, r, 1) for r in range(DEAL)]
     last = len(batches) - 1
@@ -43,8 +43,6 @@ def tile_rows_read_sig_norm_kernel(tc, q, qa, S, out):
         ctx.enter_context(tc.manual_schedule())
 
         qa_t = sb.tile([P, PACK], F32, name="qa_t")
-        for c in range(SIDE):
-            nc.scalar.dma_start(out=qa_t[ROWS * c : ROWS * (c + 1), :], in_=qa_rows)
         qa_cols = qa_t[:].rearrange("p (u e) -> p u e", e=2).unsqueeze(1).to_broadcast([P, M, 2, 2])
 
         q_raw, s_raw = {}, {}
@@ -56,18 +54,22 @@ def tile_rows_read_sig_norm_kernel(tc, q, qa, S, out):
             for u in range(2):
                 q_raw[k, u] = sb.tile([P, 2, CHUNK], F32, name="q_raw%d_%d" % (k, u))
                 nc.sync.dma_start(out=q_raw[k, u][:], in_=q_rows[g, :, u, :, n0 : n0 + CHUNK])
+            if k == 0:
+                nc.sync.dma_start(out=qa_t[:], in_=qa_rows)
 
         phi, s_bf, s_codes, s_scales = {}, {}, {}, {}
         fq, codes, scales, acc, inv, res = {}, {}, {}, {}, {}, {}
 
+        def round_state(g, copy):
+            s_bf[g] = sb.tile([P, E, PACK], BF16, name="s_bf%d" % g, align_bytes=64)
+            copy(
+                out=s_bf[g][:].rearrange("p (x i) j -> p x j i", i=2),
+                in_=s_raw[g][:].rearrange("p j (x i) -> p x j i", i=2),
+            )
+
         def feature_map(k):
-            g = k // CHUNKS_PER_PAIR
-            if k % CHUNKS_PER_PAIR == STATE_AT:
-                s_bf[g] = sb.tile([P, E, PACK], BF16, name="s_bf%d" % g, align_bytes=64)
-                nc.scalar.copy(
-                    out=s_bf[g][:].rearrange("p (x i) j -> p x j i", i=2),
-                    in_=s_raw[g][:].rearrange("p j (x i) -> p x j i", i=2),
-                )
+            if k == STATE_AT:
+                round_state(0, nc.scalar.copy)
             phi[k] = sb.tile([P, 2, CHUNK, 2], F32, name="phi%d" % k)
             for u in range(2):
                 nc.scalar.activation(out=phi[k][:, u, :, :], in_=q_raw[k, u][:].rearrange("p e n -> p n e"), func=ACT.Sigmoid)
@@ -151,6 +153,8 @@ def tile_rows_read_sig_norm_kernel(tc, q, qa, S, out):
                 multiply(b - 1)
             for i in range(1, batches[b][2]):
                 weigh(b, i)
+            if b == CHUNKS_PER_PAIR:
+                round_state(1, nc.vector.tensor_copy)
         quantize_queries(last)
         multiply(last)
         invert(last - LAG)

@@ -63,8 +63,8 @@ def tile_rows_read_sig_norm_kernel(tc, q, qa, S, out):
         def round_state(g, copy):
             s_bf[g] = sb.tile([P, E, PACK], BF16, name="s_bf%d" % g, align_bytes=64)
             copy(
-                out=s_bf[g][:].rearrange("p (x i) j -> p x j i", i=2),
-                in_=s_raw[g][:].rearrange("p j (x i) -> p x j i", i=2),
+                out=s_bf[g][:].rearrange("p (x i) j -> p x j i", i=4),
+                in_=s_raw[g][:].rearrange("p j (x i) -> p x j i", i=4),
             )
 
         def feature_map(k):
@@ -97,8 +97,8 @@ def tile_rows_read_sig_norm_kernel(tc, q, qa, S, out):
             g = k // CHUNKS_PER_PAIR
             for c in range(SIDE):
                 acc[b, c] = ps.tile([P, count, E], F32, name="acc%d_%d" % (b, c), tag="bank%d_%d" % (b % BANKS, c))
-            for c in range(SIDE):
-                for i in range(count):
+            for i in range(count):
+                for c in range(SIDE):
                     rows = slice(ROWS * c, ROWS * (c + 1))
                     cols = slice(M * i, M * (i + 1))
                     nc.tensor.matmul_mx(
@@ -113,7 +113,7 @@ def tile_rows_read_sig_norm_kernel(tc, q, qa, S, out):
 
         def invert(b):
             count = batches[b][2]
-            for c in range(SIDE):
+            for c in reversed(range(SIDE)):
                 inv[b, c] = sb.tile([P, count], F32, name="inv%d_%d" % (b, c))
                 nc.vector.reciprocal(out=inv[b, c][:], in_=acc[b, c][:, :, E - 1])
 

@@ -68,8 +68,8 @@ def tile_rows_read_sig_norm_kernel(tc, q, qa, S, out):
             )
 
         def feature_map(k):
-            if k == STATE_AT:
-                round_state(0, nc.scalar.copy)
+            if k % CHUNKS_PER_PAIR == STATE_AT:
+                round_state(k // CHUNKS_PER_PAIR, nc.scalar.copy)
             phi[k] = sb.tile([P, 2, CHUNK, 2], F32, name="phi%d" % k)
             for u in range(2):
                 nc.scalar.activation(out=phi[k][:, u, :, :], in_=q_raw[k, u][:].rearrange("p e n -> p n e"), func=ACT.Sigmoid)
@@ -144,7 +144,7 @@ def tile_rows_read_sig_norm_kernel(tc, q, qa, S, out):
                 quantize_queries(b - 1)
             if b % CHUNKS_PER_PAIR == 1:
                 quantize_state(b // CHUNKS_PER_PAIR)
-            if LAG <= b < last:
+            if b >= LAG:
                 invert(b - LAG)
                 normalise(b - LAG, False)
             if b + AHEAD < CHUNKS:
@@ -153,12 +153,9 @@ def tile_rows_read_sig_norm_kernel(tc, q, qa, S, out):
                 multiply(b - 1)
             for i in range(1, batches[b][2]):
                 weigh(b, i)
-            if b == CHUNKS_PER_PAIR:
-                round_state(1, nc.vector.tensor_copy)
         quantize_queries(last)
         multiply(last)
-        invert(last - LAG)
-        for b in range(last - LAG, last + 1):
-            if b < last:
-                invert(b + 1)
-            normalise(b, True)
+        invert(last - 1)
+        invert(last)
+        normalise(last - 1, True)
+        normalise(last, True)

from contextlib import ExitStack

import concourse.mybir as mybir

H, D, N, E = 4, 256, 1024, 128
FLOPS = 2 * H * D * N * E

F32 = mybir.dt.float32
BF16 = mybir.dt.bfloat16
U32 = mybir.dt.uint32
U8 = mybir.dt.uint8
FP8X4 = mybir.dt.float8_e4m3fn_x4
ACT = mybir.ActivationFunctionType
ALU = mybir.AluOpType

P = 128
SIDE = 2
ROWS = P // SIDE
PACK = 4
M = 128
DEAL = 2
CHUNK = M * DEAL
CHUNKS_PER_PAIR = N // CHUNK
CHUNKS = (H // SIDE) * CHUNKS_PER_PAIR
BANKS = 4
STATE_AT = 2
AHEAD = 3
LAG = 2


def tile_rows_read_sig_norm_kernel(tc, q, qa, S, out):
    nc = tc.nc
    q_rows = q.rearrange("(g c) (p u e) n -> g (c p) u e n", c=SIDE, u=2, e=2)
    s_rows = S.rearrange("(g c) (p j) e -> g (c p) j e", c=SIDE, j=PACK)
    qa_rows = qa.rearrange("(p j) o -> p (j o)", j=PACK).unsqueeze(0).to_broadcast([SIDE, ROWS, PACK])

    batches = [(k, 0, DEAL) for k in range(CHUNKS - 1)] + [(CHUNKS - 1, r, 1) for r in range(DEAL)]
    last = len(batches) - 1

    with ExitStack() as ctx:
        sb = ctx.enter_context(tc.tile_pool(name="sb", bufs=1))
        ps = ctx.enter_context(tc.psum_pool(name="ps", bufs=1))
        ctx.enter_context(tc.manual_schedule())

        qa_t = sb.tile([P, PACK], F32, name="qa_t")
        qa_cols = qa_t[:].rearrange("p (u e) -> p u e", e=2).unsqueeze(1).to_broadcast([P, M, 2, 2])

        q_raw, s_raw = {}, {}
        for k in range(CHUNKS):
            g, n0 = k // CHUNKS_PER_PAIR, CHUNK * (k % CHUNKS_PER_PAIR)
            if k % CHUNKS_PER_PAIR == STATE_AT:
                s_raw[g] = sb.tile([P, PACK, E], F32, name="s_raw%d" % g)
                nc.sync.dma_start(out=s_raw[g][:], in_=s_rows[g])
            for u in range(2):
                q_raw[k, u] = sb.tile([P, 2, CHUNK], F32, name="q_raw%d_%d" % (k, u))
                nc.sync.dma_start(out=q_raw[k, u][:], in_=q_rows[g, :, u, :, n0 : n0 + CHUNK])
            if k == 0:
                nc.sync.dma_start(out=qa_t[:], in_=qa_rows)

        phi, s_bf, s_codes, s_scales = {}, {}, {}, {}
        fq, codes, scales, acc, inv, res = {}, {}, {}, {}, {}, {}

        def round_state(g, copy):
            s_bf[g] = sb.tile([P, E, PACK], BF16, name="s_bf%d" % g, align_bytes=64)
            copy(
                out=s_bf[g][:].rearrange("p (x i) j -> p x j i", i=4),
                in_=s_raw[g][:].rearrange("p j (x i) -> p x j i", i=4),
            )

        def feature_map(k):
            if k % CHUNKS_PER_PAIR == STATE_AT:
                round_state(k // CHUNKS_PER_PAIR, nc.scalar.copy)
            phi[k] = sb.tile([P, 2, CHUNK, 2], F32, name="phi%d" % k)
            for u in range(2):
                nc.scalar.activation(out=phi[k][:, u, :, :], in_=q_raw[k, u][:].rearrange("p e n -> p n e"), func=ACT.Sigmoid)

        def weigh(b, i):
            k, r0, count = batches[b]
            if i == 0:
                fq[b] = sb.tile([P, count, M, 2, 2], BF16, name="fq%d" % b, align_bytes=64)
            dealt = phi[k][:].rearrange("p u (m r) e -> p r m u e", r=DEAL)
            nc.vector.tensor_tensor(out=fq[b][:, i, :, :, :], in0=dealt[:, r0 + i, :, :, :], in1=qa_cols, op=ALU.mult)

        def quantize_state(g):
            s_codes[g] = sb.tile([P, E], U32, name="s_codes%d" % g, align_bytes=64)
            s_scales[g] = sb.tile([P, E], U8, name="s_scales%d" % g, align_bytes=64)
            nc.vector.quantize_mx(out=s_codes[g][:].bitcast(FP8X4), scales=s_scales[g][:], in_=s_bf[g][:].rearrange("p e j -> p (e j)"))

        def quantize_queries(b):
            count = batches[b][2]
            codes[b] = sb.tile([P, count * M], U32, name="codes%d" % b, align_bytes=64)
            scales[b] = sb.tile([P, count * M], U8, name="scales%d" % b, align_bytes=64)
            nc.vector.quantize_mx(out=codes[b][:].bitcast(FP8X4), scales=scales[b][:], in_=fq[b][:].rearrange("p i m u e -> p (i m u e)"))

        def multiply(b):
            k, r0, count = batches[b]
            g = k // CHUNKS_PER_PAIR
            for c in range(SIDE):
                acc[b, c] = ps.tile([P, count, E], F32, name="acc%d_%d" % (b, c), tag="bank%d_%d" % (b % BANKS, c))
            for i in range(count):
                for c in range(SIDE):
                    rows = slice(ROWS * c, ROWS * (c + 1))
                    cols = slice(M * i, M * (i + 1))
                    nc.tensor.matmul_mx(
                        out=acc[b, c][:, i, :],
                        lhsT=codes[b][rows, cols].bitcast(FP8X4),
                        lhsT_scale=scales[b][rows, cols],
                        rhs=s_codes[g][rows, :].bitcast(FP8X4),
                        rhs_scale=s_scales[g][rows, :],
                        start=True,
                        stop=True,
                    )

        def invert(b):
            count = batches[b][2]
            for c in reversed(range(SIDE)):
                inv[b, c] = sb.tile([P, count], F32, name="inv%d_%d" % (b, c))
                nc.vector.reciprocal(out=inv[b, c][:], in_=acc[b, c][:, :, E - 1])

        def normalise(b, share):
            k, r0, count = batches[b]
            if r0 == 0:
                res[k] = sb.tile([P, SIDE, DEAL, E], F32, name="res%d" % k)
            for c in range(1 if share else SIDE):
                for i in range(count):
                    nc.scalar.activation(out=res[k][:, c, r0 + i, :], in_=acc[b, c][:, i, :], func=ACT.Copy, scale=inv[b, c][:, i : i + 1])
            if share:
                nc.vector.tensor_tensor(
                    out=res[k][:, 1, r0 : r0 + count, :],
                    in0=acc[b, 1][:],
                    in1=inv[b, 1][:].unsqueeze(2).to_broadcast([P, count, E]),
                    op=ALU.mult,
                )
            if r0 + count == DEAL:
                g, n0 = k // CHUNKS_PER_PAIR, CHUNK * (k % CHUNKS_PER_PAIR)
                rows = out[SIDE * g : SIDE * (g + 1), n0 : n0 + CHUNK, :]
                nc.sync.dma_start(out=rows.rearrange("c (m r) e -> m c (r e)", r=DEAL), in_=res[k][:].rearrange("m c r e -> m c (r e)"))

        for k in range(AHEAD):
            feature_map(k)
        for b in range(last + 1):
            weigh(b, 0)
            if b >= 1:
                quantize_queries(b - 1)
            if b % CHUNKS_PER_PAIR == 1:
                quantize_state(b // CHUNKS_PER_PAIR)
            if b >= LAG:
                invert(b - LAG)
                normalise(b - LAG, False)
            if b + AHEAD < CHUNKS:
                feature_map(b + AHEAD)
            if b >= 1:
                multiply(b - 1)
            for i in range(1, batches[b][2]):
                weigh(b, i)
        quantize_queries(last)
        multiply(last)
        invert(last - 1)
        invert(last)
        normalise(last - 1, True)
        normalise(last, True)
